import numpy as np
import ml_dtypes


def mxq(x, axis, fmt="e4m3"):
    dtype, down = {"e4m3": (ml_dtypes.float8_e4m3fn, 7), "e5m2": (ml_dtypes.float8_e5m2, 14)}[fmt]
    v = np.moveaxis(np.asarray(x, np.float32).astype(ml_dtypes.bfloat16).astype(np.float64), axis, -1)
    blocks = v.reshape(v.shape[:-1] + (-1, 32))
    amax = np.abs(blocks).max(-1, keepdims=True)
    byte = np.maximum(np.where(amax > 0, np.frexp(amax)[1] - 1 + 127, 0) - down, 1)
    scale = np.exp2(byte - 127.0)
    codes = (blocks / scale).astype(np.float32).astype(dtype).astype(np.float64)
    return np.moveaxis((codes * scale).reshape(v.shape), -1, axis)


WIDE = False


def mx_kscale(k):
    if not WIDE:
        return np.ones(k)
    levels = np.array([10, -10, 5, -5, 0])
    if k % 512:
        return np.exp2(np.random.permutation(np.resize(levels, k // 32))).repeat(32)
    a = np.empty((k // 512, 16))
    for p in range(k // 512):
        a[p, :8] = np.random.permutation(np.resize(levels, 8))
        for g in range(8):
            far = levels[np.abs(levels - a[p, g]) >= 10]
            a[p, g + 8] = far[np.random.randint(len(far))]
    return np.exp2(a.ravel()).repeat(32)


def f64(x):
    return np.asarray(x).astype(np.float64)


def striped(idx):
    return np.tile(np.asarray(idx).reshape(-1, 16).T, (8, 1)).astype(np.uint16)


def unstriped(offs):
    return offs[:16].T.reshape(-1).astype(np.int64)


def striped8(idx):
    return np.asarray(idx).reshape(8, -1, 16).transpose(0, 2, 1).reshape(128, -1).astype(np.uint16)


def unstriped8(offs):
    return offs.reshape(8, 16, -1).transpose(0, 2, 1).reshape(8, -1).astype(np.int64)


def pick8(x, idx, run):
    r = np.arange(len(x))
    return x[r[:, None], idx[r % (8 * run) // run]]


E2M1 = np.array([0.0, 0.5, 1.0, 1.5, 2.0, 3.0, 4.0, 6.0, -0.0, -0.5, -1.0, -1.5, -2.0, -3.0, -4.0, -6.0])


def pack_weight(w, fmt):
    k, n = w.shape
    w = f64(np.asarray(w, np.float32).astype(ml_dtypes.bfloat16)).reshape(k // 32, 32, n)
    amax = np.abs(w).max(1)
    if fmt == "e4m3":
        byte = np.frexp(amax)[1] - 1 + 127 - 7
    else:
        mant, ex = np.frexp(amax / 6.0)
        byte = np.where(mant > 0.5, ex, ex - 1) + 127
    byte = np.clip(np.where(amax > 0, byte, 1), 1, 254)
    scaled = (w * np.exp2(127.0 - byte)[:, None, :]).reshape(k, n).astype(np.float32)
    by_word = np.ascontiguousarray(scaled.reshape(k // 512, 128, 4, n).transpose(0, 1, 3, 2))
    if fmt == "e4m3":
        words = by_word.astype(ml_dtypes.float8_e4m3fn).view(np.uint8)
    else:
        c = by_word.astype(ml_dtypes.float4_e2m1fn).view(np.uint8) & 0xF
        words = (c[..., 0::2] | (c[..., 1::2] << 4)).reshape(k // 512, 128, 2 * n)
    return np.ascontiguousarray(words), np.ascontiguousarray(byte.astype(np.uint8).reshape(k // 512, 16, n))


def unpack_weight(words, scales, fmt):
    g, _, n = scales.shape
    words = np.ascontiguousarray(words).reshape(g, 128, n, -1)
    if fmt == "e4m3":
        vals = words.view(ml_dtypes.float8_e4m3fn).astype(np.float64)
    else:
        nib = np.empty((g, 128, n, 4), np.uint8)
        nib[..., 0::2] = words & 0xF
        nib[..., 1::2] = words >> 4
        vals = E2M1[nib]
    vals = vals * np.repeat(np.exp2(scales.astype(np.float64) - 127.0), 8, axis=1)[..., None]
    return vals.transpose(0, 1, 3, 2).reshape(g * 512, n)


K, J, R, T, F, C, O, N, U = 512, 512, 512, 1024, 1024, 1024, 256, 256, 128


def setup_inputs():
    n = np.random.standard_normal
    idx = np.random.permutation(T)[:J]
    idx2 = np.stack([np.random.permutation(F)[:R] for _ in range(8)])
    idx3 = np.random.permutation(C)[:J]
    idx4 = np.random.permutation(C)[:O]
    idx5 = np.stack([np.random.permutation(C)[:O] for _ in range(8)])
    idx6 = np.stack([np.random.permutation(O)[:U] for _ in range(8)])
    idx7 = np.stack([np.random.permutation(O)[:U] for _ in range(8)])
    fk = mx_kscale(K)
    fr = mx_kscale(R)
    xtp = pack_weight(n((K, T)) * fk[:, None], "e2m1")
    wbp = pack_weight(n((R, N)) * 1 / np.sqrt(R) / fr[:, None], "e4m3")
    wop = pack_weight(n((R, N)) * 1 / np.sqrt(R) / fr[:, None], "e2m1")
    return {
        "xt_words": xtp[0],
        "xt_scales": xtp[1],
        "ua": (np.random.randint(-7, 8, (K, F)).astype(np.float64)).astype(np.float32),
        "ha": ((np.random.randint(8, 25, (K, 1)) / 1024.0) / fk[:, None]).astype(np.float32),
        "sa": (np.random.uniform(0.5, 1.6, (R, 1)) * fr[:, None]).astype(np.float32),
        "sb": (np.random.uniform(0.5, 1.6, (R, 1)) * fr[:, None]).astype(np.float32),
        "wb_words": wbp[0],
        "wb_scales": wbp[1],
        "wo_words": wop[0],
        "wo_scales": wop[1],
        "so": (np.random.uniform(0.5, 1.6, (N, 1))).astype(np.float32),
        "sp": (np.random.uniform(0.5, 1.6, (N, 1))).astype(np.float32),
        "offs": striped(idx),
        "offs2": striped8(idx2),
        "offs3": striped(idx3),
        "offs4": striped(idx4),
        "offs5": striped8(idx5),
        "offs6": striped8(idx6),
        "offs7": striped8(idx7),
    }


def reference(xt_words, xt_scales, ua, ha, sa, sb, wb_words, wb_scales, wo_words, wo_scales, so, sp, offs, offs2, offs3, offs4, offs5, offs6, offs7):
    idx = unstriped(offs)
    idx2 = unstriped8(offs2)
    idx3 = unstriped(offs3)
    idx4 = unstriped(offs4)
    idx5 = unstriped8(offs5)
    idx6 = unstriped8(offs6)
    idx7 = unstriped8(offs7)
    xtu = unpack_weight(xt_words, xt_scales, "e2m1")
    wbu = unpack_weight(wb_words, wb_scales, "e4m3")
    wou = unpack_weight(wo_words, wo_scales, "e2m1")
    wc = pick8(f64(ua), idx2, 64) * f64(ha)
    wcq = mxq(wc, 0, "e4m3")
    xtidxg = xtu[:, idx]
    a = wcq.T @ xtidxg
    pw = np.zeros((R, C))
    pw[:, idx3] = a
    hid = np.abs(pw[:, idx4] * f64(sa) - pick8(pw, idx5, 64) * f64(sb))
    hidq = mxq(hid, 0, "e4m3")
    p = wbu.T @ hidq
    q = wou.T @ hidq
    y = pick8(p, idx6, 16) * f64(so) - pick8(q, idx7, 16) * f64(sp)
    return y

@@ -1,0 +1,233 @@
+from contextlib import ExitStack
+
+import concourse.mybir as mybir
+
+K, J, R, T, F, C, O, N, U = 512, 512, 512, 1024, 1024, 1024, 256, 256, 128
+FLOPS = 2 * K * R * J + 2 * 2 * R * N * O
+
+F32 = mybir.dt.float32
+BF16 = mybir.dt.bfloat16
+I32 = mybir.dt.int32
+U32 = mybir.dt.uint32
+U16 = mybir.dt.uint16
+U8 = mybir.dt.uint8
+FP8X4 = mybir.dt.float8_e4m3fn_x4
+FP4X4 = mybir.dt.float4_e2m1fn_x4
+ACT = mybir.ActivationFunctionType
+ALU = mybir.AluOpType
+
+P = 128
+PACK = 4
+LIST_ROWS = 16
+LAST_ON_SCALAR = 256
+
+
+def tile_picked_tokens_codes_one_boardmixed_outcomes_outmeet_kernel(
+    tc, xt_words, xt_scales, ua, ha, sa, sb, wb_words, wb_scales, wo_words, wo_scales, so, sp,
+    offs, offs2, offs3, offs4, offs5, offs6, offs7, out,
+):
+    nc = tc.nc
+    with ExitStack() as ctx:
+        lists = ctx.enter_context(tc.tile_pool(name="lists", bufs=1))
+        keep = ctx.enter_context(tc.tile_pool(name="keep", bufs=1))
+        psum = ctx.enter_context(tc.psum_pool(name="psum", bufs=1))
+
+        def load_list(name, src):
+            tile = lists.tile(list(src.shape), U16, name=name)
+            nc.sync.dma_start(tile[:], src)
+            return tile
+
+        def entries(tile, first, count):
+            return tile[:, first // LIST_ROWS : (first + count) // LIST_ROWS]
+
+        def load_by_word(name, src, queue):
+            tile = keep.tile([P, PACK], F32, name=name)
+            queue.dma_start(tile[:], src.rearrange("(p t) o -> p (t o)", t=PACK))
+            return tile
+
+        ua_rows = ua.rearrange("(p t) f -> p t f", t=PACK)
+        ua_t = [keep.tile([P, F], F32, name="ua%d" % t) for t in range(PACK)]
+        ha_t = load_by_word("ha_t", ha, nc.scalar)
+        xs_stage = keep.tile([PACK, 4, T // 4], I32, name="xs_stage")
+        nc.sync.dma_start(ua_t[0][:], ua_rows[:, 0, :])
+        l2 = load_list("l2", offs2)
+        nc.sync.dma_start(ua_t[1][:], ua_rows[:, 1, :])
+        nc.sync.dma_start(xs_stage[:], xt_scales[0].bitcast(I32).rearrange("(q i) c -> i q c", i=PACK))
+        l1 = load_list("l1", offs)
+        nc.sync.dma_start(ua_t[2][:], ua_rows[:, 2, :])
+        nc.sync.dma_start(ua_t[3][:], ua_rows[:, 3, :])
+        xw = keep.tile([P, T], U16, name="xw")
+        nc.sync.dma_start(xw[:].bitcast(I32), xt_words[0].bitcast(I32))
+        l3 = load_list("l3", offs3)
+        l4 = load_list("l4", offs4)
+        l5 = load_list("l5", offs5)
+        sa_t = load_by_word("sa_t", sa, nc.sync)
+        sb_t = load_by_word("sb_t", sb, nc.sync)
+
+        xs = keep.tile([P, T], U8, name="xs")
+        nc.vector.memset(xs[:].bitcast(I32), 0)
+        planes = []
+        for name in ("wb_plane", "wo_plane"):
+            plane = keep.tile([P, N], U8, name=name, align_bytes=64)
+            nc.vector.memset(plane[:].bitcast(I32), 0)
+            planes.append(plane)
+        wb_plane, wo_plane = planes
+        board = [keep.tile([P, C], F32, name="board%d" % s) for s in range(PACK)]
+        for s in range(PACK):
+            nc.vector.memset(board[s][:], 0.0)
+
+        wb = keep.tile([P, N], I32, name="wb", align_bytes=64)
+        nc.sync.dma_start(wb[:], wb_words[0].rearrange("p n t -> p (n t)").bitcast(I32))
+        wo = keep.tile([P, 2 * N], U8, name="wo", align_bytes=64)
+        nc.sync.dma_start(wo[:].bitcast(I32), wo_words[0].bitcast(I32))
+        for plane, src in ((wb_plane, wb_scales), (wo_plane, wo_scales)):
+            for q in range(4):
+                nc.sync.dma_start(plane[32 * q : 32 * q + 4, :].bitcast(I32), src[0, 4 * q : 4 * q + 4, :].bitcast(I32))
+        l6 = load_list("l6", offs6)
+        l7 = load_list("l7", offs7)
+        so_t, sp_t = [], []
+        for a in range(N // P):
+            for name, src, tiles in (("so", so, so_t), ("sp", sp, sp_t)):
+                col = keep.tile([P, 1], F32, name="%s%d" % (name, a))
+                nc.sync.dma_start(col[:], src[a * P : (a + 1) * P, :])
+                tiles.append(col)
+
+        for q in range(4):
+            nc.vector.tensor_copy(xs[32 * q : 32 * q + 4, :].bitcast(I32), xs_stage[:, q, :])
+        xg_scales = keep.tile([P, J], U8, name="xg_scales", align_bytes=64)
+        nc.vector.tensor_copy(xg_scales[:], xs[:].indirect(l1[:]))
+
+        def gather_words(part, tag):
+            words = keep.tile([P, J // 2], U16, name="xg_words%d" % part, tag=tag, align_bytes=64)
+            nc.vector.tensor_copy(words[:], xw[:].indirect(entries(l1, part * (J // 2), J // 2)))
+            return words
+
+        wc = keep.tile([P, PACK, R], BF16, name="wc")
+        for t in range(PACK):
+            nc.scalar.activation(
+                out=wc[:, t, :], in_=ua_t[t][:].indirect(l2[:]), func=ACT.Copy, scale=ha_t[:, t : t + 1]
+            )
+        wc_words = [keep.tile([P, P], U32, name="wc_words%d" % s, align_bytes=64) for s in range(PACK)]
+        wc_scales = [keep.tile([P, P], U8, name="wc_scales%d" % s, align_bytes=64) for s in range(PACK)]
+
+        def deal(first, count, copy):
+            dealt = keep.tile([P, count, P * PACK], BF16, name="dealt%d" % first, tag="dealt%d" % first, align_bytes=64)
+            copy(
+                dealt[:].rearrange("p s (m t) -> p m t s", t=PACK),
+                wc[:].rearrange("p t (m s) -> p m t s", s=PACK)[:, :, :, first : first + count],
+            )
+            return [dealt[:, i, :] for i in range(count)]
+
+        def quantize_wc(s, dealt):
+            nc.vector.quantize_mx(out=wc_words[s][:].bitcast(FP8X4), scales=wc_scales[s][:], in_=dealt)
+
+        xg_words = [gather_words(0, "xg_words0")]
+        dealt = deal(0, 1, nc.vector.tensor_copy) + deal(1, 1, nc.vector.tensor_copy) + deal(2, 2, nc.scalar.copy)
+        quantize_wc(0, dealt[0])
+        quantize_wc(1, dealt[1])
+        xg_words.append(gather_words(1, "dealt1"))
+        quantize_wc(2, dealt[2])
+        quantize_wc(3, dealt[3])
+
+        a_sb = [keep.tile([P, J], F32, name="a_sb%d" % s) for s in range(PACK)]
+        half = J // 2
+        a_ps = {}
+
+        def product(s, part, acc):
+            nc.tensor.matmul_mx(
+                out=acc, lhsT=wc_words[s][:].bitcast(FP8X4), lhsT_scale=wc_scales[s][:],
+                rhs=xg_words[part][:].bitcast(FP4X4), rhs_scale=xg_scales[:, part * half : (part + 1) * half],
+                start=True, stop=True,
+            )
+
+        for part in range(2):
+            for s in range(2):
+                acc = psum.tile([P, half], F32, name="a_ps%d%d" % (s, part), tag="bank%d" % (2 * part + s))
+                product(s, part, acc[:])
+                a_ps[(s, part * half)] = acc
+        for s in (3, 2):
+            acc = psum.tile([P, J], F32, name="a_ps%d" % s, tag="bank%d" % (s + 2))
+            for part in range(2):
+                product(s, part, acc[:, part * half : (part + 1) * half])
+            a_ps[(s, 0)] = acc
+
+        def leave_psum(copy, s, first, count):
+            copy(a_sb[s][:, first : first + count], a_ps[(s, first)][:])
+
+        def scatter_scalar(s, first, count):
+            nc.scalar.activation(
+                out=board[s][:].indirect(entries(l3, first, count)), in_=a_sb[s][:, first : first + count], func=ACT.Copy
+            )
+
+        def scatter_vector(s, first, count):
+            nc.vector.tensor_copy(board[s][:].indirect(entries(l3, first, count)), a_sb[s][:, first : first + count])
+
+        places = O // 2
+        diff = [keep.tile([P, PACK, places], F32, name="diff%d" % g) for g in range(2)]
+
+        def fetch(s, cuts):
+            first = keep.tile([P, O], F32, name="first%d" % s)
+            second = keep.tile([P, O], F32, name="second%d" % s)
+            nc.scalar.activation(out=second[:], in_=board[s][:].indirect(l5[:]), func=ACT.Copy, scale=sb_t[:, s : s + 1])
+            width = O // cuts
+            for c in range(cuts):
+                nc.scalar.activation(
+                    out=first[:, c * width : (c + 1) * width], in_=board[s][:].indirect(entries(l4, c * width, width)),
+                    func=ACT.Copy, scale=sa_t[:, s : s + 1],
+                )
+            for g in range(2):
+                o_cols = slice(g * places, (g + 1) * places)
+                nc.vector.tensor_tensor(diff[g][:, s, :], first[:, o_cols], second[:, o_cols], ALU.subtract)
+
+        leave_psum(nc.scalar.copy, 0, 0, J // 2)
+        leave_psum(nc.scalar.copy, 1, 0, J // 2)
+        scatter_scalar(0, 0, J // 2)
+        scatter_vector(1, 0, J // 2)
+        leave_psum(nc.scalar.copy, 0, J // 2, J // 2)
+        leave_psum(nc.vector.tensor_copy, 1, J // 2, J // 2)
+        leave_psum(nc.scalar.copy, 3, 0, J)
+        leave_psum(nc.vector.tensor_copy, 2, 0, J)
+        scatter_scalar(0, J // 2, J // 2)
+        scatter_vector(1, J // 2, J // 2)
+        scatter_scalar(3, 0, LAST_ON_SCALAR)
+        scatter_vector(2, 0, J)
+        scatter_vector(3, LAST_ON_SCALAR, J - LAST_ON_SCALAR)
+        for s in range(PACK):
+            fetch(s, 2 if s == PACK - 1 else 1)
+
+        outcome = [
+            keep.tile([P, O], F32, name="outcome%d" % i) for i in range(4)
+        ]
+        stationary = []
+        for a in range(N // P):
+            n_cols = slice(a * P, (a + 1) * P)
+            stationary.append((wb[:, n_cols].bitcast(FP8X4), wb_plane[:, n_cols]))
+            stationary.append((wo[:, 2 * a * P : 2 * (a + 1) * P].bitcast(FP4X4), wo_plane[:, n_cols]))
+        sums = []
+        for g in range(2):
+            hid = keep.tile([P, places, PACK], BF16, name="hid%d" % g, align_bytes=64)
+            nc.scalar.activation(out=hid[:], in_=diff[g][:].rearrange("p t o -> p o t"), func=ACT.Abs)
+            hid_words = keep.tile([P, places], U32, name="hid_words%d" % g, align_bytes=64)
+            hid_scales = keep.tile([P, places], U8, name="hid_scales%d" % g, align_bytes=64)
+            nc.vector.quantize_mx(
+                out=hid_words[:].bitcast(FP8X4), scales=hid_scales[:], in_=hid[:].rearrange("p o t -> p (o t)")
+            )
+            for i, (words, plane) in enumerate(stationary):
+                acc = psum.tile([P, places], F32, name="sum%d%d" % (g, i), tag="bank%d" % (4 * g + i))
+                nc.tensor.matmul_mx(
+                    out=acc[:], lhsT=words, lhsT_scale=plane,
+                    rhs=hid_words[:].bitcast(FP8X4), rhs_scale=hid_scales[:], start=True, stop=True,
+                )
+                sums.append(acc)
+        for g, copy in enumerate((nc.scalar.copy, nc.vector.tensor_copy)):
+            for i in range(4):
+                copy(outcome[i][:, g * places : (g + 1) * places], sums[4 * g + i][:])
+
+        for a in range(N // P):
+            p_got = keep.tile([P, U], F32, name="p_got%d" % a)
+            q_got = keep.tile([P, U], F32, name="q_got%d" % a)
+            nc.scalar.activation(out=p_got[:], in_=outcome[2 * a][:].indirect(l6[:]), func=ACT.Copy, scale=so_t[a][:])
+            nc.scalar.activation(out=q_got[:], in_=outcome[2 * a + 1][:].indirect(l7[:]), func=ACT.Copy, scale=sp_t[a][:])
+            y = keep.tile([P, U], F32, name="y%d" % a)
+            nc.vector.tensor_tensor(y[:], p_got[:], q_got[:], ALU.subtract)
+            nc.sync.dma_start(out[a * P : (a + 1) * P, :], y[:])

@@ -45,6 +45,11 @@ def tile_picked_tokens_codes_one_boardmixed_outcomes_outmeet_kernel(
             queue.dma_start(tile[:], src.rearrange("(p t) o -> p (t o)", t=PACK))
             return tile
 
+        warm_in = keep.tile([P, 1], F32, name="warm_in")
+        warm_out = keep.tile([P, 1], F32, name="warm_out")
+        nc.gpsimd.memset(warm_in[:], 0.0)
+        nc.scalar.activation(out=warm_out[:], in_=warm_in[:], func=ACT.Abs)
+
         ua_rows = ua.rearrange("(p t) f -> p t f", t=PACK)
         ua_t = [keep.tile([P, F], F32, name="ua%d" % t) for t in range(PACK)]
         ha_t = load_by_word("ha_t", ha, nc.scalar)

@@ -19,7 +19,7 @@ ALU = mybir.AluOpType
 P = 128
 PACK = 4
 LIST_ROWS = 16
-LAST_ON_SCALAR = 256
+LAST_ON_SCALAR = 320
 
 
 def tile_picked_tokens_codes_one_boardmixed_outcomes_outmeet_kernel(
@@ -53,13 +53,15 @@ def tile_picked_tokens_codes_one_boardmixed_outcomes_outmeet_kernel(
         ua_rows = ua.rearrange("(p t) f -> p t f", t=PACK)
         ua_t = [keep.tile([P, F], F32, name="ua%d" % t) for t in range(PACK)]
         ha_t = load_by_word("ha_t", ha, nc.scalar)
-        xs_stage = keep.tile([PACK, 4, T // 4], I32, name="xs_stage")
+        xs = keep.tile([P, T], U8, name="xs")
+        nc.gpsimd.memset(xs[:].bitcast(I32), 0)
         nc.sync.dma_start(ua_t[0][:], ua_rows[:, 0, :])
         l2 = load_list("l2", offs2)
         nc.sync.dma_start(ua_t[1][:], ua_rows[:, 1, :])
-        nc.sync.dma_start(xs_stage[:], xt_scales[0].bitcast(I32).rearrange("(q i) c -> i q c", i=PACK))
-        l1 = load_list("l1", offs)
         nc.sync.dma_start(ua_t[2][:], ua_rows[:, 2, :])
+        for i in range(4):
+            nc.sync.dma_start(xs[i:P:32, :].bitcast(I32), xt_scales[0, i:16:4, :].bitcast(I32))
+        l1 = load_list("l1", offs)
         nc.sync.dma_start(ua_t[3][:], ua_rows[:, 3, :])
         xw = keep.tile([P, T], U16, name="xw")
         nc.sync.dma_start(xw[:].bitcast(I32), xt_words[0].bitcast(I32))
@@ -69,8 +71,6 @@ def tile_picked_tokens_codes_one_boardmixed_outcomes_outmeet_kernel(
         sa_t = load_by_word("sa_t", sa, nc.sync)
         sb_t = load_by_word("sb_t", sb, nc.sync)
 
-        xs = keep.tile([P, T], U8, name="xs")
-        nc.vector.memset(xs[:].bitcast(I32), 0)
         planes = []
         for name in ("wb_plane", "wo_plane"):
             plane = keep.tile([P, N], U8, name=name, align_bytes=64)
@@ -97,8 +97,6 @@ def tile_picked_tokens_codes_one_boardmixed_outcomes_outmeet_kernel(
                 nc.sync.dma_start(col[:], src[a * P : (a + 1) * P, :])
                 tiles.append(col)
 
-        for q in range(4):
-            nc.vector.tensor_copy(xs[32 * q : 32 * q + 4, :].bitcast(I32), xs_stage[:, q, :])
         xg_scales = keep.tile([P, J], U8, name="xg_scales", align_bytes=64)
         nc.vector.tensor_copy(xg_scales[:], xs[:].indirect(l1[:]))
 
@@ -170,19 +168,24 @@ def tile_picked_tokens_codes_one_boardmixed_outcomes_outmeet_kernel(
         places = O // 2
         diff = [keep.tile([P, PACK, places], F32, name="diff%d" % g) for g in range(2)]
 
+        first = keep.tile([P, PACK, O], F32, name="first")
+        second = keep.tile([P, PACK, O], F32, name="second")
+
         def fetch(s, cuts):
-            first = keep.tile([P, O], F32, name="first%d" % s)
-            second = keep.tile([P, O], F32, name="second%d" % s)
-            nc.scalar.activation(out=second[:], in_=board[s][:].indirect(l5[:]), func=ACT.Copy, scale=sb_t[:, s : s + 1])
+            nc.scalar.activation(
+                out=second[:, s, :], in_=board[s][:].indirect(l5[:]), func=ACT.Copy, scale=sb_t[:, s : s + 1]
+            )
             width = O // cuts
             for c in range(cuts):
                 nc.scalar.activation(
-                    out=first[:, c * width : (c + 1) * width], in_=board[s][:].indirect(entries(l4, c * width, width)),
+                    out=first[:, s, c * width : (c + 1) * width], in_=board[s][:].indirect(entries(l4, c * width, width)),
                     func=ACT.Copy, scale=sa_t[:, s : s + 1],
                 )
+
+        def subtract(tiles):
             for g in range(2):
                 o_cols = slice(g * places, (g + 1) * places)
-                nc.vector.tensor_tensor(diff[g][:, s, :], first[:, o_cols], second[:, o_cols], ALU.subtract)
+                nc.vector.tensor_tensor(diff[g][:, tiles, :], first[:, tiles, o_cols], second[:, tiles, o_cols], ALU.subtract)
 
         leave_psum(nc.scalar.copy, 0, 0, J // 2)
         leave_psum(nc.scalar.copy, 1, 0, J // 2)
@@ -197,8 +200,11 @@ def tile_picked_tokens_codes_one_boardmixed_outcomes_outmeet_kernel(
         scatter_scalar(3, 0, LAST_ON_SCALAR)
         scatter_vector(2, 0, J)
         scatter_vector(3, LAST_ON_SCALAR, J - LAST_ON_SCALAR)
-        for s in range(PACK):
-            fetch(s, 2 if s == PACK - 1 else 1)
+        for s in range(PACK - 1):
+            fetch(s, 1)
+        subtract(slice(0, PACK - 1))
+        fetch(PACK - 1, 2)
+        subtract(slice(PACK - 1, PACK))
 
         outcome = [
             keep.tile([P, O], F32, name="outcome%d" % i) for i in range(4)
@@ -208,25 +214,31 @@ def tile_picked_tokens_codes_one_boardmixed_outcomes_outmeet_kernel(
             n_cols = slice(a * P, (a + 1) * P)
             stationary.append((wb[:, n_cols].bitcast(FP8X4), wb_plane[:, n_cols]))
             stationary.append((wo[:, 2 * a * P : 2 * (a + 1) * P].bitcast(FP4X4), wo_plane[:, n_cols]))
-        sums = []
+        hid_words = keep.tile([P, O], U32, name="hid_words", align_bytes=64)
+        hid_scales = keep.tile([P, O], U8, name="hid_scales", align_bytes=64)
         for g in range(2):
+            o_cols = slice(g * places, (g + 1) * places)
             hid = keep.tile([P, places, PACK], BF16, name="hid%d" % g, align_bytes=64)
-            nc.scalar.activation(out=hid[:], in_=diff[g][:].rearrange("p t o -> p o t"), func=ACT.Abs)
-            hid_words = keep.tile([P, places], U32, name="hid_words%d" % g, align_bytes=64)
-            hid_scales = keep.tile([P, places], U8, name="hid_scales%d" % g, align_bytes=64)
-            nc.vector.quantize_mx(
-                out=hid_words[:].bitcast(FP8X4), scales=hid_scales[:], in_=hid[:].rearrange("p o t -> p (o t)")
+            nc.scalar.activation(
+                out=hid[:].rearrange("p (c i) t -> p c t i", i=4),
+                in_=diff[g][:].rearrange("p t (c i) -> p c t i", i=4),
+                func=ACT.Abs,
             )
-            for i, (words, plane) in enumerate(stationary):
-                acc = psum.tile([P, places], F32, name="sum%d%d" % (g, i), tag="bank%d" % (4 * g + i))
-                nc.tensor.matmul_mx(
-                    out=acc[:], lhsT=words, lhsT_scale=plane,
-                    rhs=hid_words[:].bitcast(FP8X4), rhs_scale=hid_scales[:], start=True, stop=True,
-                )
-                sums.append(acc)
-        for g, copy in enumerate((nc.scalar.copy, nc.vector.tensor_copy)):
-            for i in range(4):
-                copy(outcome[i][:, g * places : (g + 1) * places], sums[4 * g + i][:])
+            nc.vector.quantize_mx(
+                out=hid_words[:, o_cols].bitcast(FP8X4), scales=hid_scales[:, o_cols],
+                in_=hid[:].rearrange("p o t -> p (o t)"),
+            )
+        steps = [(i, g * places, places) for g in range(2) for i in range(2)] + [(i, 0, O) for i in range(2, 4)]
+        for bank, (i, start, count) in enumerate(steps):
+            o_cols = slice(start, start + count)
+            words, plane = stationary[i]
+            acc = psum.tile([P, count], F32, name="sum%d" % bank, tag="bank%d" % bank)
+            nc.tensor.matmul_mx(
+                out=acc[:], lhsT=words, lhsT_scale=plane,
+                rhs=hid_words[:, o_cols].bitcast(FP8X4), rhs_scale=hid_scales[:, o_cols], start=True, stop=True,
+            )
+            copy = nc.scalar.copy if start + count < O else nc.vector.tensor_copy
+            copy(outcome[i][:, o_cols], acc[:])
 
         for a in range(N // P):
             p_got = keep.tile([P, U], F32, name="p_got%d" % a)

@@ -105,27 +105,37 @@ def tile_picked_tokens_codes_one_boardmixed_outcomes_outmeet_kernel(
             nc.vector.tensor_copy(words[:], xw[:].indirect(entries(l1, part * (J // 2), J // 2)))
             return words
 
-        wc = keep.tile([P, PACK, R], BF16, name="wc")
+        wc = keep.tile([P, PACK * R], BF16, name="wc")
         for t in range(PACK):
             nc.scalar.activation(
-                out=wc[:, t, :], in_=ua_t[t][:].indirect(l2[:]), func=ACT.Copy, scale=ha_t[:, t : t + 1]
+                out=wc[:, t * R : (t + 1) * R], in_=ua_t[t][:].indirect(l2[:]), func=ACT.Copy, scale=ha_t[:, t : t + 1]
             )
         wc_words = [keep.tile([P, P], U32, name="wc_words%d" % s, align_bytes=64) for s in range(PACK)]
         wc_scales = [keep.tile([P, P], U8, name="wc_scales%d" % s, align_bytes=64) for s in range(PACK)]
 
-        def deal(first, count, copy):
-            dealt = keep.tile([P, count, P * PACK], BF16, name="dealt%d" % first, tag="dealt%d" % first, align_bytes=64)
+        groups = [(0, 1), (1, 1), (2, 2)]
+        dealt_tiles = [
+            keep.tile([P, count, P * PACK], BF16, name="dealt%d" % first, tag="dealt%d" % first, align_bytes=64)
+            for first, count in groups
+        ]
+
+        def deal(planes_t, group, copy):
+            first, count = groups[group]
             copy(
-                dealt[:].rearrange("p s (m t) -> p m t s", t=PACK),
-                wc[:].rearrange("p t (m s) -> p m t s", s=PACK)[:, :, :, first : first + count],
+                dealt_tiles[group][:].rearrange("p s (m t) -> p m t s", t=PACK)[:, :, planes_t, :],
+                wc[:].rearrange("p (t m s) -> p m t s", t=PACK, s=PACK)[:, :, planes_t, first : first + count],
             )
-            return [dealt[:, i, :] for i in range(count)]
 
         def quantize_wc(s, dealt):
             nc.vector.quantize_mx(out=wc_words[s][:].bitcast(FP8X4), scales=wc_scales[s][:], in_=dealt)
 
+        for group in range(2):
+            deal(slice(0, 2), group, nc.vector.tensor_copy)
         xg_words = [gather_words(0, "xg_words0")]
-        dealt = deal(0, 1, nc.vector.tensor_copy) + deal(1, 1, nc.vector.tensor_copy) + deal(2, 2, nc.scalar.copy)
+        for group in range(2):
+            deal(slice(2, PACK), group, nc.vector.tensor_copy)
+        deal(slice(0, PACK), 2, nc.scalar.copy)
+        dealt = [dealt_tiles[0][:, 0, :], dealt_tiles[1][:, 0, :], dealt_tiles[2][:, 0, :], dealt_tiles[2][:, 1, :]]
         quantize_wc(0, dealt[0])
         quantize_wc(1, dealt[1])
         xg_words.append(gather_words(1, "dealt1"))

from contextlib import ExitStack

import concourse.mybir as mybir

K, J, R, T, F, C, O, N, U = 512, 512, 512, 1024, 1024, 1024, 256, 256, 128
FLOPS = 2 * K * R * J + 2 * 2 * R * N * O

F32 = mybir.dt.float32
BF16 = mybir.dt.bfloat16
I32 = mybir.dt.int32
U32 = mybir.dt.uint32
U16 = mybir.dt.uint16
U8 = mybir.dt.uint8
FP8X4 = mybir.dt.float8_e4m3fn_x4
FP4X4 = mybir.dt.float4_e2m1fn_x4
ACT = mybir.ActivationFunctionType
ALU = mybir.AluOpType

P = 128
PACK = 4
LIST_ROWS = 16
LAST_ON_SCALAR = 320


def tile_picked_tokens_codes_one_boardmixed_outcomes_outmeet_kernel(
    tc, xt_words, xt_scales, ua, ha, sa, sb, wb_words, wb_scales, wo_words, wo_scales, so, sp,
    offs, offs2, offs3, offs4, offs5, offs6, offs7, out,
):
    nc = tc.nc
    with ExitStack() as ctx:
        lists = ctx.enter_context(tc.tile_pool(name="lists", bufs=1))
        keep = ctx.enter_context(tc.tile_pool(name="keep", bufs=1))
        psum = ctx.enter_context(tc.psum_pool(name="psum", bufs=1))

        def load_list(name, src):
            tile = lists.tile(list(src.shape), U16, name=name)
            nc.sync.dma_start(tile[:], src)
            return tile

        def entries(tile, first, count):
            return tile[:, first // LIST_ROWS : (first + count) // LIST_ROWS]

        def load_by_word(name, src, queue):
            tile = keep.tile([P, PACK], F32, name=name)
            queue.dma_start(tile[:], src.rearrange("(p t) o -> p (t o)", t=PACK))
            return tile

        warm_in = keep.tile([P, 1], F32, name="warm_in")
        warm_out = keep.tile([P, 1], F32, name="warm_out")
        nc.gpsimd.memset(warm_in[:], 0.0)
        nc.scalar.activation(out=warm_out[:], in_=warm_in[:], func=ACT.Abs)

        ua_rows = ua.rearrange("(p t) f -> p t f", t=PACK)
        ua_t = [keep.tile([P, F], F32, name="ua%d" % t) for t in range(PACK)]
        ha_t = load_by_word("ha_t", ha, nc.scalar)
        xs = keep.tile([P, T], U8, name="xs")
        nc.gpsimd.memset(xs[:].bitcast(I32), 0)
        nc.sync.dma_start(ua_t[0][:], ua_rows[:, 0, :])
        l2 = load_list("l2", offs2)
        nc.sync.dma_start(ua_t[1][:], ua_rows[:, 1, :])
        nc.sync.dma_start(ua_t[2][:], ua_rows[:, 2, :])
        for i in range(4):
            nc.sync.dma_start(xs[i:P:32, :].bitcast(I32), xt_scales[0, i:16:4, :].bitcast(I32))
        l1 = load_list("l1", offs)
        nc.sync.dma_start(ua_t[3][:], ua_rows[:, 3, :])
        xw = keep.tile([P, T], U16, name="xw")
        nc.sync.dma_start(xw[:].bitcast(I32), xt_words[0].bitcast(I32))
        l3 = load_list("l3", offs3)
        l4 = load_list("l4", offs4)
        l5 = load_list("l5", offs5)
        sa_t = load_by_word("sa_t", sa, nc.sync)
        sb_t = load_by_word("sb_t", sb, nc.sync)

        planes = []
        for name in ("wb_plane", "wo_plane"):
            plane = keep.tile([P, N], U8, name=name, align_bytes=64)
            nc.vector.memset(plane[:].bitcast(I32), 0)
            planes.append(plane)
        wb_plane, wo_plane = planes
        board = [keep.tile([P, C], F32, name="board%d" % s) for s in range(PACK)]
        for s in range(PACK):
            nc.vector.memset(board[s][:], 0.0)

        wb = keep.tile([P, N], I32, name="wb", align_bytes=64)
        nc.sync.dma_start(wb[:], wb_words[0].rearrange("p n t -> p (n t)").bitcast(I32))
        wo = keep.tile([P, 2 * N], U8, name="wo", align_bytes=64)
        nc.sync.dma_start(wo[:].bitcast(I32), wo_words[0].bitcast(I32))
        for plane, src in ((wb_plane, wb_scales), (wo_plane, wo_scales)):
            for q in range(4):
                nc.sync.dma_start(plane[32 * q : 32 * q + 4, :].bitcast(I32), src[0, 4 * q : 4 * q + 4, :].bitcast(I32))
        l6 = load_list("l6", offs6)
        l7 = load_list("l7", offs7)
        so_t, sp_t = [], []
        for a in range(N // P):
            for name, src, tiles in (("so", so, so_t), ("sp", sp, sp_t)):
                col = keep.tile([P, 1], F32, name="%s%d" % (name, a))
                nc.sync.dma_start(col[:], src[a * P : (a + 1) * P, :])
                tiles.append(col)

        xg_scales = keep.tile([P, J], U8, name="xg_scales", align_bytes=64)
        nc.vector.tensor_copy(xg_scales[:], xs[:].indirect(l1[:]))

        def gather_words(part, tag):
            words = keep.tile([P, J // 2], U16, name="xg_words%d" % part, tag=tag, align_bytes=64)
            nc.vector.tensor_copy(words[:], xw[:].indirect(entries(l1, part * (J // 2), J // 2)))
            return words

        wc = keep.tile([P, PACK * R], BF16, name="wc")
        for t in range(PACK):
            nc.scalar.activation(
                out=wc[:, t * R : (t + 1) * R], in_=ua_t[t][:].indirect(l2[:]), func=ACT.Copy, scale=ha_t[:, t : t + 1]
            )
        wc_words = [keep.tile([P, P], U32, name="wc_words%d" % s, align_bytes=64) for s in range(PACK)]
        wc_scales = [keep.tile([P, P], U8, name="wc_scales%d" % s, align_bytes=64) for s in range(PACK)]

        groups = [(0, 1), (1, 1), (2, 2)]
        dealt_tiles = [
            keep.tile([P, count, P * PACK], BF16, name="dealt%d" % first, tag="dealt%d" % first, align_bytes=64)
            for first, count in groups
        ]

        def deal(planes_t, group, copy):
            first, count = groups[group]
            copy(
                dealt_tiles[group][:].rearrange("p s (m t) -> p m t s", t=PACK)[:, :, planes_t, :],
                wc[:].rearrange("p (t m s) -> p m t s", t=PACK, s=PACK)[:, :, planes_t, first : first + count],
            )

        def quantize_wc(s, dealt):
            nc.vector.quantize_mx(out=wc_words[s][:].bitcast(FP8X4), scales=wc_scales[s][:], in_=dealt)

        for group in range(2):
            deal(slice(0, 2), group, nc.vector.tensor_copy)
        xg_words = [gather_words(0, "xg_words0")]
        for group in range(2):
            deal(slice(2, PACK), group, nc.vector.tensor_copy)
        deal(slice(0, PACK), 2, nc.scalar.copy)
        dealt = [dealt_tiles[0][:, 0, :], dealt_tiles[1][:, 0, :], dealt_tiles[2][:, 0, :], dealt_tiles[2][:, 1, :]]
        quantize_wc(0, dealt[0])
        quantize_wc(1, dealt[1])
        xg_words.append(gather_words(1, "dealt1"))
        quantize_wc(2, dealt[2])
        quantize_wc(3, dealt[3])

        a_sb = [keep.tile([P, J], F32, name="a_sb%d" % s) for s in range(PACK)]
        half = J // 2
        a_ps = {}

        def product(s, part, acc):
            nc.tensor.matmul_mx(
                out=acc, lhsT=wc_words[s][:].bitcast(FP8X4), lhsT_scale=wc_scales[s][:],
                rhs=xg_words[part][:].bitcast(FP4X4), rhs_scale=xg_scales[:, part * half : (part + 1) * half],
                start=True, stop=True,
            )

        for part in range(2):
            for s in range(2):
                acc = psum.tile([P, half], F32, name="a_ps%d%d" % (s, part), tag="bank%d" % (2 * part + s))
                product(s, part, acc[:])
                a_ps[(s, part * half)] = acc
        for s in (3, 2):
            acc = psum.tile([P, J], F32, name="a_ps%d" % s, tag="bank%d" % (s + 2))
            for part in range(2):
                product(s, part, acc[:, part * half : (part + 1) * half])
            a_ps[(s, 0)] = acc

        def leave_psum(copy, s, first, count):
            copy(a_sb[s][:, first : first + count], a_ps[(s, first)][:])

        def scatter_scalar(s, first, count):
            nc.scalar.activation(
                out=board[s][:].indirect(entries(l3, first, count)), in_=a_sb[s][:, first : first + count], func=ACT.Copy
            )

        def scatter_vector(s, first, count):
            nc.vector.tensor_copy(board[s][:].indirect(entries(l3, first, count)), a_sb[s][:, first : first + count])

        places = O // 2
        diff = [keep.tile([P, PACK, places], F32, name="diff%d" % g) for g in range(2)]

        first = keep.tile([P, PACK, O], F32, name="first")
        second = keep.tile([P, PACK, O], F32, name="second")

        def fetch(s, cuts):
            nc.scalar.activation(
                out=second[:, s, :], in_=board[s][:].indirect(l5[:]), func=ACT.Copy, scale=sb_t[:, s : s + 1]
            )
            width = O // cuts
            for c in range(cuts):
                nc.scalar.activation(
                    out=first[:, s, c * width : (c + 1) * width], in_=board[s][:].indirect(entries(l4, c * width, width)),
                    func=ACT.Copy, scale=sa_t[:, s : s + 1],
                )

        def subtract(tiles):
            for g in range(2):
                o_cols = slice(g * places, (g + 1) * places)
                nc.vector.tensor_tensor(diff[g][:, tiles, :], first[:, tiles, o_cols], second[:, tiles, o_cols], ALU.subtract)

        leave_psum(nc.scalar.copy, 0, 0, J // 2)
        leave_psum(nc.scalar.copy, 1, 0, J // 2)
        scatter_scalar(0, 0, J // 2)
        scatter_vector(1, 0, J // 2)
        leave_psum(nc.scalar.copy, 0, J // 2, J // 2)
        leave_psum(nc.vector.tensor_copy, 1, J // 2, J // 2)
        leave_psum(nc.scalar.copy, 3, 0, J)
        leave_psum(nc.vector.tensor_copy, 2, 0, J)
        scatter_scalar(0, J // 2, J // 2)
        scatter_vector(1, J // 2, J // 2)
        scatter_scalar(3, 0, LAST_ON_SCALAR)
        scatter_vector(2, 0, J)
        scatter_vector(3, LAST_ON_SCALAR, J - LAST_ON_SCALAR)
        for s in range(PACK - 1):
            fetch(s, 1)
        subtract(slice(0, PACK - 1))
        fetch(PACK - 1, 2)
        subtract(slice(PACK - 1, PACK))

        outcome = [
            keep.tile([P, O], F32, name="outcome%d" % i) for i in range(4)
        ]
        stationary = []
        for a in range(N // P):
            n_cols = slice(a * P, (a + 1) * P)
            stationary.append((wb[:, n_cols].bitcast(FP8X4), wb_plane[:, n_cols]))
            stationary.append((wo[:, 2 * a * P : 2 * (a + 1) * P].bitcast(FP4X4), wo_plane[:, n_cols]))
        hid_words = keep.tile([P, O], U32, name="hid_words", align_bytes=64)
        hid_scales = keep.tile([P, O], U8, name="hid_scales", align_bytes=64)
        for g in range(2):
            o_cols = slice(g * places, (g + 1) * places)
            hid = keep.tile([P, places, PACK], BF16, name="hid%d" % g, align_bytes=64)
            nc.scalar.activation(
                out=hid[:].rearrange("p (c i) t -> p c t i", i=4),
                in_=diff[g][:].rearrange("p t (c i) -> p c t i", i=4),
                func=ACT.Abs,
            )
            nc.vector.quantize_mx(
                out=hid_words[:, o_cols].bitcast(FP8X4), scales=hid_scales[:, o_cols],
                in_=hid[:].rearrange("p o t -> p (o t)"),
            )
        steps = [(i, g * places, places) for g in range(2) for i in range(2)] + [(i, 0, O) for i in range(2, 4)]
        for bank, (i, start, count) in enumerate(steps):
            o_cols = slice(start, start + count)
            words, plane = stationary[i]
            acc = psum.tile([P, count], F32, name="sum%d" % bank, tag="bank%d" % bank)
            nc.tensor.matmul_mx(
                out=acc[:], lhsT=words, lhsT_scale=plane,
                rhs=hid_words[:, o_cols].bitcast(FP8X4), rhs_scale=hid_scales[:, o_cols], start=True, stop=True,
            )
            copy = nc.scalar.copy if start + count < O else nc.vector.tensor_copy
            copy(outcome[i][:, o_cols], acc[:])

        for a in range(N // P):
            p_got = keep.tile([P, U], F32, name="p_got%d" % a)
            q_got = keep.tile([P, U], F32, name="q_got%d" % a)
            nc.scalar.activation(out=p_got[:], in_=outcome[2 * a][:].indirect(l6[:]), func=ACT.Copy, scale=so_t[a][:])
            nc.scalar.activation(out=q_got[:], in_=outcome[2 * a + 1][:].indirect(l7[:]), func=ACT.Copy, scale=sp_t[a][:])
            y = keep.tile([P, U], F32, name="y%d" % a)
            nc.vector.tensor_tensor(y[:], p_got[:], q_got[:], ALU.subtract)
            nc.sync.dma_start(out[a * P : (a + 1) * P, :], y[:])
